import numpy as np
import ml_dtypes


def mxq(x, axis, fmt="e4m3"):
    dtype, down = {"e4m3": (ml_dtypes.float8_e4m3fn, 7), "e5m2": (ml_dtypes.float8_e5m2, 14)}[fmt]
    v = np.moveaxis(np.asarray(x, np.float32).astype(ml_dtypes.bfloat16).astype(np.float64), axis, -1)
    blocks = v.reshape(v.shape[:-1] + (-1, 32))
    amax = np.abs(blocks).max(-1, keepdims=True)
    byte = np.maximum(np.where(amax > 0, np.frexp(amax)[1] - 1 + 127, 0) - down, 1)
    scale = np.exp2(byte - 127.0)
    codes = (blocks / scale).astype(np.float32).astype(dtype).astype(np.float64)
    return np.moveaxis((codes * scale).reshape(v.shape), -1, axis)


WIDE = False


def mx_kscale(k):
    if not WIDE:
        return np.ones(k)
    levels = np.array([10, -10, 5, -5, 0])
    if k % 512:
        return np.exp2(np.random.permutation(np.resize(levels, k // 32))).repeat(32)
    a = np.empty((k // 512, 16))
    for p in range(k // 512):
        a[p, :8] = np.random.permutation(np.resize(levels, 8))
        for g in range(8):
            far = levels[np.abs(levels - a[p, g]) >= 10]
            a[p, g + 8] = far[np.random.randint(len(far))]
    return np.exp2(a.ravel()).repeat(32)


def f64(x):
    return np.asarray(x).astype(np.float64)


def striped(idx):
    return np.tile(idx.reshape(-1, 16).T, (8, 1)).astype(np.uint16)


def unstriped(offs):
    return offs[:16].T.reshape(-1).astype(np.int64)


def striped8(idx):
    return np.concatenate([x.reshape(-1, 16).T for x in idx]).astype(np.uint16)


def runs(offs, k):
    lists = np.stack([offs[16 * r : 16 * r + 16].T.reshape(-1) for r in range(8)]).astype(np.int64)
    return lists[np.arange(k) % 512 // 64]


def pack_weight(w):
    k, n = w.shape
    w = f64(np.asarray(w, np.float32).astype(ml_dtypes.bfloat16)).reshape(k // 32, 32, n)
    amax = np.abs(w).max(1)
    byte = np.clip(np.where(amax > 0, np.frexp(amax)[1] - 1 + 127 - 7, 1), 1, 254)
    scaled = (w * np.exp2(127.0 - byte)[:, None, :]).reshape(k, n).astype(np.float32)
    words = np.ascontiguousarray(scaled.reshape(k // 512, 128, 4, n).transpose(0, 1, 3, 2)).astype(ml_dtypes.float8_e4m3fn).view(np.uint8)
    return words, np.ascontiguousarray(byte.astype(np.uint8).reshape(k // 512, 16, n))


def unpack_weight(words, scales):
    g, p, n, _ = words.shape
    vals = np.ascontiguousarray(words).view(ml_dtypes.float8_e4m3fn).astype(np.float64) * np.repeat(np.exp2(scales.astype(np.float64) - 127.0), 8, axis=1)[..., None]
    return vals.transpose(0, 1, 3, 2).reshape(g * 512, n)


def sigmoid(v):
    return 1.0 / (1.0 + np.exp(-np.maximum(v, -700.0)))


K, T, S, H, C = 512, 2048, 512, 512, 512


def setup_inputs():
    n = np.random.standard_normal
    s = mx_kscale(K)[:, None]
    packed_xT = pack_weight(n((K, T)) * s)
    return {
        "x_words": packed_xT[0],
        "x_scales": packed_xT[1],
        "w1": (n((K, H)) / np.sqrt(K) / s).astype(np.float32),
        "tau": np.random.uniform(0.3, 0.9, (H, 1)).astype(np.float32),
        "gs": (np.random.uniform(0.5, 1.5, (K, 1)) / s).astype(np.float32),
        "sl": np.random.uniform(1.5, 3.0, (C, 1)).astype(np.float32),
        "th": (0.5 * n((C, 1))).astype(np.float32),
        "offs": striped(np.random.permutation(T)[:S]),
        "n1": striped(np.random.permutation(S)),
        "n2": striped(np.random.permutation(S)),
        "cand": striped(np.random.permutation(T)[:C]),
        "n3": striped8(np.stack([np.random.permutation(S) for _ in range(8)])),
        "n4": striped8(np.stack([np.random.permutation(S) for _ in range(8)])),
    }


def reference(x_words, x_scales, w1, tau, gs, sl, th, offs, n1, n2, cand, n3, n4):
    x_cand = unpack_weight(x_words, x_scales)[:, unstriped(cand)]
    xq = unpack_weight(x_words, x_scales)[:, unstriped(offs)]
    y = mxq(f64(w1), 0, "e4m3").T @ xq
    top = y.max(axis=1, keepdims=True)
    ea = np.exp(f64(tau) * (y[:, unstriped(n1)] - top))
    sm = y * ea
    ds = np.zeros((H, S))
    ds[:, unstriped(n2)] = sm
    z = f64(gs) * (2.0 * ds - (0.5 * y))
    s = 0.0625 * ((x_cand.T @ mxq(z, 0, "e4m3")))
    sg = sigmoid(f64(sl) * (s[np.arange(C)[:, None], runs(n3, C)] - f64(th)))
    return 1.5 * (s * (sg - (sg[np.arange(C)[:, None], runs(n4, C)])))

@@ -1,0 +1,220 @@
+from contextlib import ExitStack
+
+import concourse.mybir as mybir
+
+K, T, S, H, C = 512, 2048, 512, 512, 512
+FLOPS = 2 * K * H * S + 2 * K * C * S
+
+F32 = mybir.dt.float32
+BF16 = mybir.dt.bfloat16
+I32 = mybir.dt.int32
+U32 = mybir.dt.uint32
+U16 = mybir.dt.uint16
+U8 = mybir.dt.uint8
+FP8X4 = mybir.dt.float8_e4m3fn_x4
+ALU = mybir.AluOpType
+ACT = mybir.ActivationFunctionType
+
+P = 128
+PACK = 4
+HALF = S // 2
+LIST_COLS = S // 16
+SCALAR_SCATTER_TILES = (1, 2)
+SCALAR_WEAVE_COLS = 160
+
+
+def halves():
+    return [(slice(h * HALF, (h + 1) * HALF), slice(h * LIST_COLS // 2, (h + 1) * LIST_COLS // 2)) for h in range(2)]
+
+
+def tile_picked_candesdedb_none_p_kernel(
+    tc, x_words, x_scales, w1, tau, gs, sl, th, offs, n1, n2, cand, n3, n4, out
+):
+    nc = tc.nc
+    with ExitStack() as ctx:
+        keep = ctx.enter_context(tc.tile_pool(name="keep", bufs=1))
+        psum = ctx.enter_context(tc.psum_pool(name="psum", bufs=1))
+
+        def load_list(src, name):
+            dst = keep.tile([P, LIST_COLS], U16, name=name)
+            nc.sync.dma_start(dst[:], src)
+            return dst
+
+        def load_rows(src, name):
+            dst = keep.tile([P, PACK], F32, name=name)
+            nc.sync.dma_start(dst[:], src.rearrange("(p t) o -> p (t o)", t=PACK))
+            return dst
+
+        table_scales = keep.tile([P, T], U8, name="table_scales", align_bytes=64)
+        nc.vector.memset(table_scales[:].bitcast(I32), 0)
+        offs_sb = load_list(offs, "offs_sb")
+        cand_sb = load_list(cand, "cand_sb")
+        for q in range(4):
+            nc.sync.dma_start(
+                table_scales[32 * q : 32 * q + 4, :].bitcast(I32), x_scales[0, 4 * q : 4 * q + 4, :].bitcast(I32)
+            )
+        table_words = keep.tile([P, T], U32, name="table_words", align_bytes=64)
+        nc.sync.dma_start(table_words[:].bitcast(I32), x_words[0].rearrange("p n t -> p (n t)").bitcast(I32))
+        w_rows = w1.rearrange("(p j) c -> p j c", j=PACK)
+        w_raw = []
+        for h in range(2):
+            part = keep.tile([P, PACK, H // 2], F32, name=f"w_raw{h}")
+            nc.sync.dma_start(part[:], w_rows[:, :, h * H // 2 : (h + 1) * H // 2])
+            w_raw.append(part)
+        tau_sb = load_rows(tau, "tau_sb")
+        n1_sb = load_list(n1, "n1_sb")
+        gs_sb = load_rows(gs, "gs_sb")
+        n2_sb = load_list(n2, "n2_sb")
+        sl_sb = load_rows(sl, "sl_sb")
+        th_sb = load_rows(th, "th_sb")
+        n3_sb = load_list(n3, "n3_sb")
+        n4_sb = load_list(n4, "n4_sb")
+
+        xq_scales = keep.tile([P, S], U8, name="xq_scales", align_bytes=64)
+        xq_words = keep.tile([P, S], U32, name="xq_words", align_bytes=64)
+        xc_scales = keep.tile([P, C], U8, name="xc_scales", align_bytes=64)
+        xc_words = keep.tile([P, C], U32, name="xc_words", align_bytes=64)
+        nc.vector.tensor_copy(xq_scales[:], table_scales[:].indirect(offs_sb[:]))
+        nc.vector.tensor_copy(
+            xc_scales[:].rearrange("p (t m) -> p m t", t=PACK), table_scales[:].indirect(cand_sb[:])
+        )
+        nc.vector.tensor_copy(xq_words[:], table_words[:].indirect(offs_sb[:]))
+        nc.vector.tensor_copy(
+            xc_words[:].rearrange("p (t m) -> p m t", t=PACK), table_words[:].indirect(cand_sb[:])
+        )
+
+        w_woven = keep.tile([P, PACK, P, PACK], BF16, name="w_woven", align_bytes=64)
+        for h, copy in enumerate((nc.scalar.copy, nc.vector.tensor_copy)):
+            copy(
+                w_woven[:, :, h * P // 2 : (h + 1) * P // 2, :].rearrange("p t m j -> p m j t"),
+                w_raw[h][:].rearrange("p j (m t) -> p m j t", t=PACK),
+            )
+        w_words = keep.tile([P, H], U32, name="w_words", align_bytes=64)
+        w_scales = keep.tile([P, H], U8, name="w_scales", align_bytes=64)
+
+        half_gs = keep.tile([P, PACK], F32, name="half_gs")
+        twice_gs = keep.tile([P, PACK], F32, name="twice_gs")
+        sig_bias = keep.tile([P, PACK], F32, name="sig_bias")
+        nc.gpsimd.tensor_scalar(half_gs[:], gs_sb[:], 0.5, 0.0, ALU.mult, ALU.add)
+        nc.gpsimd.tensor_scalar(twice_gs[:], gs_sb[:], 2.0, 0.0, ALU.mult, ALU.add)
+        minus_th = keep.tile([P, PACK], F32, name="minus_th")
+        nc.gpsimd.tensor_scalar(minus_th[:], th_sb[:], -1.0, 0.0, ALU.mult, ALU.add)
+        nc.gpsimd.tensor_tensor(sig_bias[:], minus_th[:], sl_sb[:], ALU.mult)
+
+        y_bank = [psum.tile([P, S], F32, name=f"y_bank{t}") for t in range(PACK)]
+        for t in range(PACK):
+            cols = slice(t * P, (t + 1) * P)
+            nc.vector.quantize_mx(
+                out=w_words[:, cols].bitcast(FP8X4),
+                scales=w_scales[:, cols],
+                in_=w_woven[:, t, :, :].rearrange("p m j -> p (m j)"),
+            )
+            nc.tensor.matmul_mx(
+                out=y_bank[t][:],
+                lhsT=w_words[:, cols].bitcast(FP8X4),
+                lhsT_scale=w_scales[:, cols],
+                rhs=xq_words[:].bitcast(FP8X4),
+                rhs_scale=xq_scales[:],
+                start=True,
+                stop=True,
+            )
+
+        y = [keep.tile([P, S], F32, name=f"y{t}") for t in range(PACK)]
+        ea = [keep.tile([P, S], F32, name=f"ea{t}") for t in range(PACK)]
+        ds = [keep.tile([P, S], F32, name=f"ds{t}") for t in range(PACK)]
+        for t in range(PACK):
+            top = keep.tile([P, 1], F32, name=f"top{t}")
+            exp_bias = keep.tile([P, 1], F32, name=f"exp_bias{t}")
+            nc.vector.tensor_scalar(y[t][:], y_bank[t][:], 1.0, None, ALU.mult, ALU.max, accum_out=top[:])
+            nc.gpsimd.tensor_scalar(exp_bias[:], top[:], tau_sb[:, t : t + 1], -1.0, ALU.mult, ALU.mult)
+            for cols, entries in halves():
+                nc.scalar.activation(
+                    ea[t][:, cols],
+                    y[t][:].indirect(n1_sb[:, entries]),
+                    ACT.Exp,
+                    bias=exp_bias[:],
+                    scale=tau_sb[:, t : t + 1],
+                )
+
+        z_rows = keep.tile([P, PACK, S], BF16, name="z_rows", align_bytes=64)
+
+        def scatter(t):
+            if t in SCALAR_SCATTER_TILES:
+                sm = keep.tile([P, S], F32, name=f"sm{t}")
+                nc.vector.tensor_tensor(sm[:], y[t][:], ea[t][:], ALU.mult)
+                for cols, entries in halves():
+                    nc.scalar.activation(ds[t][:].indirect(n2_sb[:, entries]), sm[:, cols], ACT.Copy)
+            else:
+                for cols, entries in halves():
+                    nc.vector.tensor_tensor(
+                        ds[t][:].indirect(n2_sb[:, entries]), y[t][:, cols], ea[t][:, cols], ALU.mult
+                    )
+
+        def combine(t):
+            y_part = keep.tile([P, S], F32, name=f"y_part{t}")
+            nc.vector.tensor_scalar(y_part[:], y[t][:], half_gs[:, t : t + 1], None, ALU.mult)
+            nc.vector.scalar_tensor_tensor(
+                z_rows[:, t, :], ds[t][:], twice_gs[:, t : t + 1], y_part[:], ALU.mult, ALU.subtract
+            )
+
+        scatter(1)
+        scatter(2)
+        scatter(0)
+        scatter(3)
+        for t in (0, 1, 3, 2):
+            combine(t)
+
+        z_woven = keep.tile([P, S, PACK], BF16, name="z_woven", align_bytes=64)
+        for cols, copy in (
+            (slice(0, SCALAR_WEAVE_COLS), nc.scalar.copy),
+            (slice(SCALAR_WEAVE_COLS, S), nc.vector.tensor_copy),
+        ):
+            copy(z_woven[:, cols, :], z_rows[:, :, cols].rearrange("p t c -> p c t"))
+        z_words = keep.tile([P, S], U32, name="z_words", align_bytes=64)
+        z_scales = keep.tile([P, S], U8, name="z_scales", align_bytes=64)
+        nc.vector.quantize_mx(
+            out=z_words[:].bitcast(FP8X4), scales=z_scales[:], in_=z_woven[:].rearrange("p c t -> p (c t)")
+        )
+
+        s_bank = [psum.tile([P, S], F32, name=f"s_bank{t}") for t in range(PACK)]
+        s = [keep.tile([P, S], F32, name=f"s{t}") for t in range(PACK)]
+        for t in range(PACK):
+            cols = slice(t * P, (t + 1) * P)
+            nc.tensor.matmul_mx(
+                out=s_bank[t][:],
+                lhsT=xc_words[:, cols].bitcast(FP8X4),
+                lhsT_scale=xc_scales[:, cols],
+                rhs=z_words[:].bitcast(FP8X4),
+                rhs_scale=z_scales[:],
+                start=True,
+                stop=True,
+            )
+            if t < PACK - 1:
+                nc.vector.tensor_scalar(s[t][:], s_bank[t][:], 0.0625, None, ALU.mult)
+            else:
+                nc.scalar.activation(s[t][:], s_bank[t][:], ACT.Copy, scale=0.0625)
+
+        out_rows = out.rearrange("(p t) c -> p t c", t=PACK)
+        for t in range(PACK):
+            sg = keep.tile([P, S], F32, name=f"sg{t}")
+            sg_again = keep.tile([P, S], F32, name=f"sg_again{t}")
+            diff = keep.tile([P, S], F32, name=f"diff{t}")
+            res = keep.tile([P, S], F32, name=f"res{t}")
+            for cols, entries in halves():
+                nc.scalar.activation(
+                    sg[:, cols],
+                    s[t][:].indirect(n3_sb[:, entries]),
+                    ACT.Sigmoid,
+                    bias=sig_bias[:, t : t + 1],
+                    scale=sl_sb[:, t : t + 1],
+                )
+            if t == 0:
+                nc.vector.tensor_copy(sg_again[:], sg[:])
+            else:
+                nc.scalar.copy(sg_again[:], sg[:])
+            for cols, entries in halves():
+                nc.vector.tensor_tensor(
+                    diff[:, cols], sg[:].indirect(n4_sb[:, entries]), sg_again[:, cols], ALU.subtract
+                )
+            nc.vector.scalar_tensor_tensor(res[:], diff[:], -1.5, s[t][:], ALU.mult, ALU.mult)
+            nc.sync.dma_start(out_rows[:, t, :], res[:])

@@ -20,7 +20,7 @@ PACK = 4
 HALF = S // 2
 LIST_COLS = S // 16
 SCALAR_SCATTER_TILES = (1, 2)
-SCALAR_WEAVE_COLS = 160
+SCALAR_WEAVE_COLS = 192
 
 
 def halves():
@@ -49,18 +49,16 @@ def tile_picked_candesdedb_none_p_kernel(
         nc.vector.memset(table_scales[:].bitcast(I32), 0)
         offs_sb = load_list(offs, "offs_sb")
         cand_sb = load_list(cand, "cand_sb")
+        w_rows = w1.rearrange("(p j) c -> p j c", j=PACK)
+        w_raw = [keep.tile([P, PACK, H // 2], F32, name=f"w_raw{h}") for h in range(2)]
+        table_words = keep.tile([P, T], U32, name="table_words", align_bytes=64)
+        nc.sync.dma_start(w_raw[0][:], w_rows[:, :, : H // 2])
         for q in range(4):
             nc.sync.dma_start(
                 table_scales[32 * q : 32 * q + 4, :].bitcast(I32), x_scales[0, 4 * q : 4 * q + 4, :].bitcast(I32)
             )
-        table_words = keep.tile([P, T], U32, name="table_words", align_bytes=64)
+        nc.sync.dma_start(w_raw[1][:], w_rows[:, :, H // 2 :])
         nc.sync.dma_start(table_words[:].bitcast(I32), x_words[0].rearrange("p n t -> p (n t)").bitcast(I32))
-        w_rows = w1.rearrange("(p j) c -> p j c", j=PACK)
-        w_raw = []
-        for h in range(2):
-            part = keep.tile([P, PACK, H // 2], F32, name=f"w_raw{h}")
-            nc.sync.dma_start(part[:], w_rows[:, :, h * H // 2 : (h + 1) * H // 2])
-            w_raw.append(part)
         tau_sb = load_rows(tau, "tau_sb")
         n1_sb = load_list(n1, "n1_sb")
         gs_sb = load_rows(gs, "gs_sb")
@@ -78,14 +76,10 @@ def tile_picked_candesdedb_none_p_kernel(
         nc.vector.tensor_copy(
             xc_scales[:].rearrange("p (t m) -> p m t", t=PACK), table_scales[:].indirect(cand_sb[:])
         )
-        nc.vector.tensor_copy(xq_words[:], table_words[:].indirect(offs_sb[:]))
-        nc.vector.tensor_copy(
-            xc_words[:].rearrange("p (t m) -> p m t", t=PACK), table_words[:].indirect(cand_sb[:])
-        )
 
         w_woven = keep.tile([P, PACK, P, PACK], BF16, name="w_woven", align_bytes=64)
-        for h, copy in enumerate((nc.scalar.copy, nc.vector.tensor_copy)):
-            copy(
+        for h in range(2):
+            nc.scalar.copy(
                 w_woven[:, :, h * P // 2 : (h + 1) * P // 2, :].rearrange("p t m j -> p m j t"),
                 w_raw[h][:].rearrange("p j (m t) -> p m j t", t=PACK),
             )
@@ -94,14 +88,15 @@ def tile_picked_candesdedb_none_p_kernel(
 
         half_gs = keep.tile([P, PACK], F32, name="half_gs")
         twice_gs = keep.tile([P, PACK], F32, name="twice_gs")
+        minus_tau = keep.tile([P, PACK], F32, name="minus_tau")
+        minus_th = keep.tile([P, PACK], F32, name="minus_th")
         sig_bias = keep.tile([P, PACK], F32, name="sig_bias")
+        nc.gpsimd.tensor_scalar(minus_tau[:], tau_sb[:], -1.0, 0.0, ALU.mult, ALU.add)
         nc.gpsimd.tensor_scalar(half_gs[:], gs_sb[:], 0.5, 0.0, ALU.mult, ALU.add)
         nc.gpsimd.tensor_scalar(twice_gs[:], gs_sb[:], 2.0, 0.0, ALU.mult, ALU.add)
-        minus_th = keep.tile([P, PACK], F32, name="minus_th")
         nc.gpsimd.tensor_scalar(minus_th[:], th_sb[:], -1.0, 0.0, ALU.mult, ALU.add)
         nc.gpsimd.tensor_tensor(sig_bias[:], minus_th[:], sl_sb[:], ALU.mult)
 
-        y_bank = [psum.tile([P, S], F32, name=f"y_bank{t}") for t in range(PACK)]
         for t in range(PACK):
             cols = slice(t * P, (t + 1) * P)
             nc.vector.quantize_mx(
@@ -109,6 +104,14 @@ def tile_picked_candesdedb_none_p_kernel(
                 scales=w_scales[:, cols],
                 in_=w_woven[:, t, :, :].rearrange("p m j -> p (m j)"),
             )
+        nc.vector.tensor_copy(xq_words[:], table_words[:].indirect(offs_sb[:]))
+        nc.vector.tensor_copy(
+            xc_words[:].rearrange("p (t m) -> p m t", t=PACK), table_words[:].indirect(cand_sb[:])
+        )
+
+        y_bank = [psum.tile([P, S], F32, name=f"y_bank{t}", tag=f"bank{t}") for t in range(PACK)]
+        for t in range(PACK):
+            cols = slice(t * P, (t + 1) * P)
             nc.tensor.matmul_mx(
                 out=y_bank[t][:],
                 lhsT=w_words[:, cols].bitcast(FP8X4),
@@ -121,12 +124,16 @@ def tile_picked_candesdedb_none_p_kernel(
 
         y = [keep.tile([P, S], F32, name=f"y{t}") for t in range(PACK)]
         ea = [keep.tile([P, S], F32, name=f"ea{t}") for t in range(PACK)]
+        sm = [keep.tile([P, S], F32, name=f"sm{t}") for t in range(PACK)]
         ds = [keep.tile([P, S], F32, name=f"ds{t}") for t in range(PACK)]
+        y_part = [keep.tile([P, S], F32, name=f"y_part{t}") for t in range(PACK)]
         for t in range(PACK):
             top = keep.tile([P, 1], F32, name=f"top{t}")
             exp_bias = keep.tile([P, 1], F32, name=f"exp_bias{t}")
             nc.vector.tensor_scalar(y[t][:], y_bank[t][:], 1.0, None, ALU.mult, ALU.max, accum_out=top[:])
-            nc.gpsimd.tensor_scalar(exp_bias[:], top[:], tau_sb[:, t : t + 1], -1.0, ALU.mult, ALU.mult)
+            nc.scalar.activation(exp_bias[:], top[:], ACT.Copy, scale=minus_tau[:, t : t + 1])
+            if t < PACK - 1:
+                nc.gpsimd.tensor_scalar(y_part[t][:], y[t][:], half_gs[:, t : t + 1], 0.0, ALU.mult, ALU.add)
             for cols, entries in halves():
                 nc.scalar.activation(
                     ea[t][:, cols],
@@ -138,83 +145,129 @@ def tile_picked_candesdedb_none_p_kernel(
 
         z_rows = keep.tile([P, PACK, S], BF16, name="z_rows", align_bytes=64)
 
-        def scatter(t):
-            if t in SCALAR_SCATTER_TILES:
-                sm = keep.tile([P, S], F32, name=f"sm{t}")
-                nc.vector.tensor_tensor(sm[:], y[t][:], ea[t][:], ALU.mult)
-                for cols, entries in halves():
-                    nc.scalar.activation(ds[t][:].indirect(n2_sb[:, entries]), sm[:, cols], ACT.Copy)
-            else:
-                for cols, entries in halves():
-                    nc.vector.tensor_tensor(
-                        ds[t][:].indirect(n2_sb[:, entries]), y[t][:, cols], ea[t][:, cols], ALU.mult
-                    )
+        def scatter_on_vector(t, h):
+            cols, entries = halves()[h]
+            nc.vector.tensor_tensor(ds[t][:].indirect(n2_sb[:, entries]), y[t][:, cols], ea[t][:, cols], ALU.mult)
 
-        def combine(t):
-            y_part = keep.tile([P, S], F32, name=f"y_part{t}")
-            nc.vector.tensor_scalar(y_part[:], y[t][:], half_gs[:, t : t + 1], None, ALU.mult)
+        def scatter_on_scalar(t, h):
+            cols, entries = halves()[h]
+            nc.scalar.activation(ds[t][:].indirect(n2_sb[:, entries]), sm[t][:, cols], ACT.Copy)
+
+        def combine(t, cols):
             nc.vector.scalar_tensor_tensor(
-                z_rows[:, t, :], ds[t][:], twice_gs[:, t : t + 1], y_part[:], ALU.mult, ALU.subtract
+                z_rows[:, t, cols], ds[t][:, cols], twice_gs[:, t : t + 1], y_part[t][:, cols], ALU.mult, ALU.subtract
             )
 
-        scatter(1)
-        scatter(2)
-        scatter(0)
-        scatter(3)
-        for t in (0, 1, 3, 2):
-            combine(t)
+        nc.vector.tensor_tensor(sm[0][:], y[0][:], ea[0][:], ALU.mult)
+        nc.vector.tensor_scalar(y_part[3][:], y[3][:], half_gs[:, 3:4], None, ALU.mult)
+        nc.vector.tensor_tensor(sm[1][:], y[1][:], ea[1][:], ALU.mult)
+        for h in range(2):
+            for t in (0, 1):
+                scatter_on_scalar(t, h)
+        for h in range(2):
+            for t in (2, 3):
+                scatter_on_vector(t, h)
+        for t in (2, 3, 0):
+            combine(t, slice(0, S))
+        for cols, entries in halves():
+            combine(1, cols)
 
         z_woven = keep.tile([P, S, PACK], BF16, name="z_woven", align_bytes=64)
-        for cols, copy in (
-            (slice(0, SCALAR_WEAVE_COLS), nc.scalar.copy),
-            (slice(SCALAR_WEAVE_COLS, S), nc.vector.tensor_copy),
-        ):
-            copy(z_woven[:, cols, :], z_rows[:, :, cols].rearrange("p t c -> p c t"))
         z_words = keep.tile([P, S], U32, name="z_words", align_bytes=64)
         z_scales = keep.tile([P, S], U8, name="z_scales", align_bytes=64)
-        nc.vector.quantize_mx(
-            out=z_words[:].bitcast(FP8X4), scales=z_scales[:], in_=z_woven[:].rearrange("p c t -> p (c t)")
-        )
-
-        s_bank = [psum.tile([P, S], F32, name=f"s_bank{t}") for t in range(PACK)]
         s = [keep.tile([P, S], F32, name=f"s{t}") for t in range(PACK)]
-        for t in range(PACK):
-            cols = slice(t * P, (t + 1) * P)
+
+        def weave(copy, c0, c1):
+            copy(
+                z_woven[:, c0:c1, :].rearrange("p (c i) t -> p c t i", i=4),
+                z_rows[:, :, c0:c1].rearrange("p t (c i) -> p c t i", i=4),
+            )
+
+        def score(t, cols, bank):
+            rows = slice(t * P, (t + 1) * P)
+            acc = psum.tile([P, cols.stop - cols.start], F32, name=f"s_bank{bank}", tag=f"bank{bank}")
             nc.tensor.matmul_mx(
-                out=s_bank[t][:],
-                lhsT=xc_words[:, cols].bitcast(FP8X4),
-                lhsT_scale=xc_scales[:, cols],
-                rhs=z_words[:].bitcast(FP8X4),
-                rhs_scale=z_scales[:],
+                out=acc[:],
+                lhsT=xc_words[:, rows].bitcast(FP8X4),
+                lhsT_scale=xc_scales[:, rows],
+                rhs=z_words[:, cols].bitcast(FP8X4),
+                rhs_scale=z_scales[:, cols],
                 start=True,
                 stop=True,
             )
-            if t < PACK - 1:
-                nc.vector.tensor_scalar(s[t][:], s_bank[t][:], 0.0625, None, ALU.mult)
-            else:
-                nc.scalar.activation(s[t][:], s_bank[t][:], ACT.Copy, scale=0.0625)
+            return acc
+
+        weave(nc.scalar.copy, 0, SCALAR_WEAVE_COLS)
+        weave(nc.vector.tensor_copy, HALF, S)
+        weave(nc.vector.tensor_copy, SCALAR_WEAVE_COLS, HALF)
+        first_banks = []
+        for h, (cols, entries) in enumerate(reversed(halves())):
+            nc.vector.quantize_mx(
+                out=z_words[:, cols].bitcast(FP8X4),
+                scales=z_scales[:, cols],
+                in_=z_woven[:, cols, :].rearrange("p c t -> p (c t)"),
+            )
+            first_banks.append((cols, score(0, cols, h)))
+        s_bank = {t: score(t, slice(0, S), PACK + t) for t in range(1, PACK)}
 
         out_rows = out.rearrange("(p t) c -> p t c", t=PACK)
-        for t in range(PACK):
-            sg = keep.tile([P, S], F32, name=f"sg{t}")
-            sg_again = keep.tile([P, S], F32, name=f"sg_again{t}")
-            diff = keep.tile([P, S], F32, name=f"diff{t}")
-            res = keep.tile([P, S], F32, name=f"res{t}")
+        sg = [keep.tile([P, S], F32, name=f"sg{t}") for t in range(PACK)]
+        other = [keep.tile([P, S], F32, name=f"other{t}") for t in range(PACK)]
+        diff = [keep.tile([P, S], F32, name=f"diff{t}") for t in range(PACK)]
+        res = [keep.tile([P, S], F32, name=f"res{t}") for t in range(PACK)]
+
+        def sigmoid(t):
             for cols, entries in halves():
                 nc.scalar.activation(
-                    sg[:, cols],
+                    sg[t][:, cols],
                     s[t][:].indirect(n3_sb[:, entries]),
                     ACT.Sigmoid,
                     bias=sig_bias[:, t : t + 1],
                     scale=sl_sb[:, t : t + 1],
                 )
-            if t == 0:
-                nc.vector.tensor_copy(sg_again[:], sg[:])
-            else:
-                nc.scalar.copy(sg_again[:], sg[:])
+
+        def fetch_and_subtract(t, h):
+            cols, entries = halves()[h]
+            nc.vector.tensor_tensor(
+                diff[t][:, cols], sg[t][:].indirect(n4_sb[:, entries]), other[t][:, cols], ALU.subtract
+            )
+
+        def duplicate(t):
             for cols, entries in halves():
-                nc.vector.tensor_tensor(
-                    diff[:, cols], sg[:].indirect(n4_sb[:, entries]), sg_again[:, cols], ALU.subtract
-                )
-            nc.vector.scalar_tensor_tensor(res[:], diff[:], -1.5, s[t][:], ALU.mult, ALU.mult)
-            nc.sync.dma_start(out_rows[:, t, :], res[:])
+                nc.vector.tensor_copy(other[t][:, cols], sg[t][:, cols])
+
+        def subtract(t, h):
+            cols, entries = halves()[h]
+            nc.vector.tensor_tensor(diff[t][:, cols], other[t][:, cols], sg[t][:, cols], ALU.subtract)
+
+        def finish(t, cols):
+            nc.vector.scalar_tensor_tensor(res[t][:, cols], diff[t][:, cols], -1.5, s[t][:, cols], ALU.mult, ALU.mult)
+            nc.sync.dma_start(out_rows[:, t, cols], res[t][:, cols])
+
+        for cols, acc in first_banks:
+            nc.vector.tensor_scalar(s[0][:, cols], acc[:], 0.0625, None, ALU.mult)
+        for t in range(1, PACK - 1):
+            nc.vector.tensor_scalar(s[t][:], s_bank[t][:], 0.0625, None, ALU.mult)
+        sigmoid(0)
+        sigmoid(1)
+        nc.scalar.activation(s[3][:], s_bank[3][:], ACT.Copy, scale=0.0625)
+        sigmoid(2)
+        nc.scalar.copy(other[2][:], sg[2][:])
+        sigmoid(3)
+        for cols, entries in halves():
+            nc.scalar.activation(other[3][:, cols], sg[3][:].indirect(n4_sb[:, entries]), ACT.Copy)
+        duplicate(0)
+        fetch_and_subtract(0, 0)
+        fetch_and_subtract(0, 1)
+        duplicate(1)
+        finish(0, slice(0, S))
+        fetch_and_subtract(1, 0)
+        fetch_and_subtract(1, 1)
+        fetch_and_subtract(2, 0)
+        finish(1, slice(0, S))
+        fetch_and_subtract(2, 1)
+        subtract(3, 0)
+        finish(2, slice(0, S))
+        subtract(3, 1)
+        for cols, entries in halves():
+            finish(3, cols)

@@ -198,6 +198,8 @@ def tile_picked_candesdedb_none_p_kernel(
             return acc
 
         weave(nc.scalar.copy, 0, SCALAR_WEAVE_COLS)
+        warm = keep.tile([P, 1], F32, name="warm")
+        nc.scalar.activation(warm[:], z_woven[:, 0, 0:1], ACT.Sigmoid)
         weave(nc.vector.tensor_copy, HALF, S)
         weave(nc.vector.tensor_copy, SCALAR_WEAVE_COLS, HALF)
         first_banks = []

@@ -17,14 +17,19 @@ ACT = mybir.ActivationFunctionType
 
 P = 128
 PACK = 4
+QUADRANTS = 4
+LIST_ROWS = 16
+WIDE = 2 * S
 HALF = S // 2
-LIST_COLS = S // 16
-SCALAR_SCATTER_TILES = (1, 2)
+LOW, HIGH, ALL = slice(0, HALF), slice(HALF, S), slice(0, S)
+LAST = PACK - 1
+VECTOR_SCATTER_SHARE = 128
 SCALAR_WEAVE_COLS = 192
+WEAVE_RUN = 4
 
 
-def halves():
-    return [(slice(h * HALF, (h + 1) * HALF), slice(h * LIST_COLS // 2, (h + 1) * LIST_COLS // 2)) for h in range(2)]
+def entries(list_tile, cols):
+    return list_tile[:, cols.start // LIST_ROWS : cols.stop // LIST_ROWS]
 
 
 def tile_picked_candesdedb_none_p_kernel(
@@ -36,11 +41,11 @@ def tile_picked_candesdedb_none_p_kernel(
         psum = ctx.enter_context(tc.psum_pool(name="psum", bufs=1))
 
         def load_list(src, name):
-            dst = keep.tile([P, LIST_COLS], U16, name=name)
+            dst = keep.tile([P, S // LIST_ROWS], U16, name=name)
             nc.sync.dma_start(dst[:], src)
             return dst
 
-        def load_rows(src, name):
+        def load_row_values(src, name):
             dst = keep.tile([P, PACK], F32, name=name)
             nc.sync.dma_start(dst[:], src.rearrange("(p t) o -> p (t o)", t=PACK))
             return dst
@@ -53,18 +58,18 @@ def tile_picked_candesdedb_none_p_kernel(
         w_raw = [keep.tile([P, PACK, H // 2], F32, name=f"w_raw{h}") for h in range(2)]
         table_words = keep.tile([P, T], U32, name="table_words", align_bytes=64)
         nc.sync.dma_start(w_raw[0][:], w_rows[:, :, : H // 2])
-        for q in range(4):
+        for q in range(QUADRANTS):
             nc.sync.dma_start(
                 table_scales[32 * q : 32 * q + 4, :].bitcast(I32), x_scales[0, 4 * q : 4 * q + 4, :].bitcast(I32)
             )
         nc.sync.dma_start(w_raw[1][:], w_rows[:, :, H // 2 :])
         nc.sync.dma_start(table_words[:].bitcast(I32), x_words[0].rearrange("p n t -> p (n t)").bitcast(I32))
-        tau_sb = load_rows(tau, "tau_sb")
+        tau_sb = load_row_values(tau, "tau_sb")
         n1_sb = load_list(n1, "n1_sb")
-        gs_sb = load_rows(gs, "gs_sb")
+        gs_sb = load_row_values(gs, "gs_sb")
         n2_sb = load_list(n2, "n2_sb")
-        sl_sb = load_rows(sl, "sl_sb")
-        th_sb = load_rows(th, "th_sb")
+        sl_sb = load_row_values(sl, "sl_sb")
+        th_sb = load_row_values(th, "th_sb")
         n3_sb = load_list(n3, "n3_sb")
         n4_sb = load_list(n4, "n4_sb")
 
@@ -98,10 +103,10 @@ def tile_picked_candesdedb_none_p_kernel(
         nc.gpsimd.tensor_tensor(sig_bias[:], minus_th[:], sl_sb[:], ALU.mult)
 
         for t in range(PACK):
-            cols = slice(t * P, (t + 1) * P)
+            places = slice(t * P, (t + 1) * P)
             nc.vector.quantize_mx(
-                out=w_words[:, cols].bitcast(FP8X4),
-                scales=w_scales[:, cols],
+                out=w_words[:, places].bitcast(FP8X4),
+                scales=w_scales[:, places],
                 in_=w_woven[:, t, :, :].rearrange("p m j -> p (m j)"),
             )
         nc.vector.tensor_copy(xq_words[:], table_words[:].indirect(offs_sb[:]))
@@ -111,85 +116,82 @@ def tile_picked_candesdedb_none_p_kernel(
 
         y_bank = [psum.tile([P, S], F32, name=f"y_bank{t}", tag=f"bank{t}") for t in range(PACK)]
         for t in range(PACK):
-            cols = slice(t * P, (t + 1) * P)
+            places = slice(t * P, (t + 1) * P)
             nc.tensor.matmul_mx(
                 out=y_bank[t][:],
-                lhsT=w_words[:, cols].bitcast(FP8X4),
-                lhsT_scale=w_scales[:, cols],
+                lhsT=w_words[:, places].bitcast(FP8X4),
+                lhsT_scale=w_scales[:, places],
                 rhs=xq_words[:].bitcast(FP8X4),
                 rhs_scale=xq_scales[:],
                 start=True,
                 stop=True,
             )
 
-        y = [keep.tile([P, S], F32, name=f"y{t}") for t in range(PACK)]
-        ea = [keep.tile([P, S], F32, name=f"ea{t}") for t in range(PACK)]
-        sm = [keep.tile([P, S], F32, name=f"sm{t}") for t in range(PACK)]
-        ds = [keep.tile([P, S], F32, name=f"ds{t}") for t in range(PACK)]
-        y_part = [keep.tile([P, S], F32, name=f"y_part{t}") for t in range(PACK)]
+        y = [keep.tile([P, WIDE], F32, name=f"y{t}") for t in range(PACK)]
+        ea = [keep.tile([P, S], F32, name=f"ea{t}", tag=f"ea{t}", align_bytes=64) for t in range(PACK)]
+        ds = [keep.tile([P, S if t in (1, 2) else WIDE], F32, name=f"ds{t}") for t in range(PACK)]
+        y_part = [keep.tile([P, S], F32, name=f"y_part{t}") for t in range(LAST)]
         for t in range(PACK):
             top = keep.tile([P, 1], F32, name=f"top{t}")
             exp_bias = keep.tile([P, 1], F32, name=f"exp_bias{t}")
-            nc.vector.tensor_scalar(y[t][:], y_bank[t][:], 1.0, None, ALU.mult, ALU.max, accum_out=top[:])
+            nc.vector.tensor_scalar(y[t][:, ALL], y_bank[t][:], 1.0, None, ALU.mult, ALU.max, accum_out=top[:])
             nc.scalar.activation(exp_bias[:], top[:], ACT.Copy, scale=minus_tau[:, t : t + 1])
-            if t < PACK - 1:
-                nc.gpsimd.tensor_scalar(y_part[t][:], y[t][:], half_gs[:, t : t + 1], 0.0, ALU.mult, ALU.add)
-            for cols, entries in halves():
-                nc.scalar.activation(
-                    ea[t][:, cols],
-                    y[t][:].indirect(n1_sb[:, entries]),
-                    ACT.Exp,
-                    bias=exp_bias[:],
-                    scale=tau_sb[:, t : t + 1],
-                )
+            if t < LAST:
+                nc.gpsimd.tensor_scalar(y_part[t][:], y[t][:, ALL], half_gs[:, t : t + 1], 0.0, ALU.mult, ALU.add)
+            nc.scalar.activation(
+                ea[t][:], y[t][:].indirect(n1_sb[:]), ACT.Exp, bias=exp_bias[:], scale=tau_sb[:, t : t + 1]
+            )
 
-        z_rows = keep.tile([P, PACK, S], BF16, name="z_rows", align_bytes=64)
+        def scatter_on_vector(t, cols):
+            nc.vector.tensor_tensor(ds[t][:].indirect(entries(n2_sb, cols)), y[t][:, cols], ea[t][:, cols], ALU.mult)
 
-        def scatter_on_vector(t, h):
-            cols, entries = halves()[h]
-            nc.vector.tensor_tensor(ds[t][:].indirect(n2_sb[:, entries]), y[t][:, cols], ea[t][:, cols], ALU.mult)
+        def product(t, cols):
+            sm = keep.tile([P, S], F32, name=f"sm{t}")
+            nc.vector.tensor_tensor(sm[:, cols], y[t][:, cols], ea[t][:, cols], ALU.mult)
+            return sm
 
-        def scatter_on_scalar(t, h):
-            cols, entries = halves()[h]
-            nc.scalar.activation(ds[t][:].indirect(n2_sb[:, entries]), sm[t][:, cols], ACT.Copy)
+        def scatter_on_scalar(t, sm, first):
+            for cols in (slice(first, HALF), HIGH):
+                nc.scalar.activation(ds[t][:].indirect(entries(n2_sb, cols)), sm[:, cols], ACT.Copy)
+
+        scatter_on_vector(0, ALL)
+        scatter_on_scalar(1, product(1, ALL), 0)
+        sm2 = product(2, slice(VECTOR_SCATTER_SHARE, S))
+        scatter_on_vector(2, slice(0, VECTOR_SCATTER_SHARE))
+        scatter_on_scalar(2, sm2, VECTOR_SCATTER_SHARE)
+        scatter_on_vector(LAST, ALL)
 
         def combine(t, cols):
             nc.vector.scalar_tensor_tensor(
                 z_rows[:, t, cols], ds[t][:, cols], twice_gs[:, t : t + 1], y_part[t][:, cols], ALU.mult, ALU.subtract
             )
 
-        nc.vector.tensor_tensor(sm[0][:], y[0][:], ea[0][:], ALU.mult)
-        nc.vector.tensor_scalar(y_part[3][:], y[3][:], half_gs[:, 3:4], None, ALU.mult)
-        nc.vector.tensor_tensor(sm[1][:], y[1][:], ea[1][:], ALU.mult)
-        for h in range(2):
-            for t in (0, 1):
-                scatter_on_scalar(t, h)
-        for h in range(2):
-            for t in (2, 3):
-                scatter_on_vector(t, h)
-        for t in (2, 3, 0):
-            combine(t, slice(0, S))
-        for cols, entries in halves():
-            combine(1, cols)
+        y_part.append(keep.tile([P, S], F32, name="y_part3", tag="ea1", align_bytes=64))
+        nc.vector.tensor_scalar(y_part[LAST][:], y[LAST][:, ALL], half_gs[:, LAST : LAST + 1], None, ALU.mult)
+        z_rows = keep.tile([P, PACK, S], BF16, name="z_rows", tag="ea2", align_bytes=64)
+        for t in (0, LAST, 1):
+            combine(t, ALL)
+        for cols in (LOW, HIGH):
+            combine(2, cols)
 
         z_woven = keep.tile([P, S, PACK], BF16, name="z_woven", align_bytes=64)
         z_words = keep.tile([P, S], U32, name="z_words", align_bytes=64)
         z_scales = keep.tile([P, S], U8, name="z_scales", align_bytes=64)
-        s = [keep.tile([P, S], F32, name=f"s{t}") for t in range(PACK)]
+        s = [keep.tile([P, WIDE], F32, name=f"s{t}") for t in range(PACK)]
 
         def weave(copy, c0, c1):
             copy(
-                z_woven[:, c0:c1, :].rearrange("p (c i) t -> p c t i", i=4),
-                z_rows[:, :, c0:c1].rearrange("p t (c i) -> p c t i", i=4),
+                z_woven[:, c0:c1, :].rearrange("p (c i) t -> p c t i", i=WEAVE_RUN),
+                z_rows[:, :, c0:c1].rearrange("p t (c i) -> p c t i", i=WEAVE_RUN),
             )
 
         def score(t, cols, bank):
-            rows = slice(t * P, (t + 1) * P)
+            places = slice(t * P, (t + 1) * P)
             acc = psum.tile([P, cols.stop - cols.start], F32, name=f"s_bank{bank}", tag=f"bank{bank}")
             nc.tensor.matmul_mx(
                 out=acc[:],
-                lhsT=xc_words[:, rows].bitcast(FP8X4),
-                lhsT_scale=xc_scales[:, rows],
+                lhsT=xc_words[:, places].bitcast(FP8X4),
+                lhsT_scale=xc_scales[:, places],
                 rhs=z_words[:, cols].bitcast(FP8X4),
                 rhs_scale=z_scales[:, cols],
                 start=True,
@@ -198,49 +200,43 @@ def tile_picked_candesdedb_none_p_kernel(
             return acc
 
         weave(nc.scalar.copy, 0, SCALAR_WEAVE_COLS)
-        warm = keep.tile([P, 1], F32, name="warm")
-        nc.scalar.activation(warm[:], z_woven[:, 0, 0:1], ACT.Sigmoid)
+        warm_up = keep.tile([P, 1], F32, name="warm_up")
+        nc.scalar.activation(warm_up[:], z_woven[:, 0, 0:1], ACT.Sigmoid)
         weave(nc.vector.tensor_copy, HALF, S)
         weave(nc.vector.tensor_copy, SCALAR_WEAVE_COLS, HALF)
         first_banks = []
-        for h, (cols, entries) in enumerate(reversed(halves())):
+        for bank, cols in enumerate((HIGH, LOW)):
             nc.vector.quantize_mx(
                 out=z_words[:, cols].bitcast(FP8X4),
                 scales=z_scales[:, cols],
                 in_=z_woven[:, cols, :].rearrange("p c t -> p (c t)"),
             )
-            first_banks.append((cols, score(0, cols, h)))
-        s_bank = {t: score(t, slice(0, S), PACK + t) for t in range(1, PACK)}
+            first_banks.append((cols, score(0, cols, bank)))
+        s_bank = {t: score(t, ALL, PACK + t) for t in range(1, PACK)}
 
         out_rows = out.rearrange("(p t) c -> p t c", t=PACK)
-        sg = [keep.tile([P, S], F32, name=f"sg{t}") for t in range(PACK)]
-        other = [keep.tile([P, S], F32, name=f"other{t}") for t in range(PACK)]
+        sg = [keep.tile([P, WIDE], F32, name=f"sg{t}") for t in range(PACK)]
+        sg2_duplicate = keep.tile([P, S], F32, name="sg2_duplicate")
+        sg3_fetched = keep.tile([P, S], F32, name="sg3_fetched")
         diff = [keep.tile([P, S], F32, name=f"diff{t}") for t in range(PACK)]
         res = [keep.tile([P, S], F32, name=f"res{t}") for t in range(PACK)]
 
-        def sigmoid(t):
-            for cols, entries in halves():
-                nc.scalar.activation(
-                    sg[t][:, cols],
-                    s[t][:].indirect(n3_sb[:, entries]),
-                    ACT.Sigmoid,
-                    bias=sig_bias[:, t : t + 1],
-                    scale=sl_sb[:, t : t + 1],
-                )
-
-        def fetch_and_subtract(t, h):
-            cols, entries = halves()[h]
-            nc.vector.tensor_tensor(
-                diff[t][:, cols], sg[t][:].indirect(n4_sb[:, entries]), other[t][:, cols], ALU.subtract
+        def sigmoid(t, cols):
+            nc.scalar.activation(
+                sg[t][:, cols],
+                s[t][:].indirect(entries(n3_sb, cols)),
+                ACT.Sigmoid,
+                bias=sig_bias[:, t : t + 1],
+                scale=sl_sb[:, t : t + 1],
             )
 
-        def duplicate(t):
-            for cols, entries in halves():
-                nc.vector.tensor_copy(other[t][:, cols], sg[t][:, cols])
+        def fetch_and_subtract(t, duplicate, cols):
+            nc.vector.tensor_tensor(
+                diff[t][:, cols], sg[t][:].indirect(entries(n4_sb, cols)), duplicate[:, cols], ALU.subtract
+            )
 
-        def subtract(t, h):
-            cols, entries = halves()[h]
-            nc.vector.tensor_tensor(diff[t][:, cols], other[t][:, cols], sg[t][:, cols], ALU.subtract)
+        def subtract_last(cols):
+            nc.vector.tensor_tensor(diff[LAST][:, cols], sg3_fetched[:, cols], sg[LAST][:, cols], ALU.subtract)
 
         def finish(t, cols):
             nc.vector.scalar_tensor_tensor(res[t][:, cols], diff[t][:, cols], -1.5, s[t][:, cols], ALU.mult, ALU.mult)
@@ -248,28 +244,31 @@ def tile_picked_candesdedb_none_p_kernel(
 
         for cols, acc in first_banks:
             nc.vector.tensor_scalar(s[0][:, cols], acc[:], 0.0625, None, ALU.mult)
-        for t in range(1, PACK - 1):
-            nc.vector.tensor_scalar(s[t][:], s_bank[t][:], 0.0625, None, ALU.mult)
-        sigmoid(0)
-        sigmoid(1)
-        nc.scalar.activation(s[3][:], s_bank[3][:], ACT.Copy, scale=0.0625)
-        sigmoid(2)
-        nc.scalar.copy(other[2][:], sg[2][:])
-        sigmoid(3)
-        for cols, entries in halves():
-            nc.scalar.activation(other[3][:, cols], sg[3][:].indirect(n4_sb[:, entries]), ACT.Copy)
-        duplicate(0)
-        fetch_and_subtract(0, 0)
-        fetch_and_subtract(0, 1)
-        duplicate(1)
-        finish(0, slice(0, S))
-        fetch_and_subtract(1, 0)
-        fetch_and_subtract(1, 1)
-        fetch_and_subtract(2, 0)
-        finish(1, slice(0, S))
-        fetch_and_subtract(2, 1)
-        subtract(3, 0)
-        finish(2, slice(0, S))
-        subtract(3, 1)
-        for cols, entries in halves():
-            finish(3, cols)
+        for t in range(1, LAST):
+            nc.vector.tensor_scalar(s[t][:, ALL], s_bank[t][:], 0.0625, None, ALU.mult)
+        for cols in (LOW, HIGH):
+            sigmoid(0, cols)
+        sigmoid(1, ALL)
+        sigmoid(2, ALL)
+        nc.scalar.activation(s[LAST][:, ALL], s_bank[LAST][:], ACT.Copy, scale=0.0625)
+        nc.scalar.copy(sg2_duplicate[:], sg[2][:, ALL])
+        sigmoid(LAST, ALL)
+        for cols in (LOW, HIGH):
+            nc.scalar.activation(sg3_fetched[:, cols], sg[LAST][:].indirect(entries(n4_sb, cols)), ACT.Copy)
+
+        sg0_duplicate = keep.tile([P, S], F32, name="sg0_duplicate", tag="vector_duplicate")
+        for cols in (LOW, HIGH):
+            nc.vector.tensor_copy(sg0_duplicate[:, cols], sg[0][:, cols])
+        for cols in (LOW, HIGH):
+            fetch_and_subtract(0, sg0_duplicate, cols)
+        sg1_duplicate = keep.tile([P, S], F32, name="sg1_duplicate", tag="vector_duplicate")
+        nc.vector.tensor_copy(sg1_duplicate[:], sg[1][:, ALL])
+        finish(0, ALL)
+        fetch_and_subtract(1, sg1_duplicate, ALL)
+        fetch_and_subtract(2, sg2_duplicate, ALL)
+        finish(1, ALL)
+        subtract_last(LOW)
+        finish(2, ALL)
+        subtract_last(HIGH)
+        for cols in (LOW, HIGH):
+            finish(LAST, cols)

from contextlib import ExitStack

import concourse.mybir as mybir

K, T, S, H, C = 512, 2048, 512, 512, 512
FLOPS = 2 * K * H * S + 2 * K * C * S

F32 = mybir.dt.float32
BF16 = mybir.dt.bfloat16
I32 = mybir.dt.int32
U32 = mybir.dt.uint32
U16 = mybir.dt.uint16
U8 = mybir.dt.uint8
FP8X4 = mybir.dt.float8_e4m3fn_x4
ALU = mybir.AluOpType
ACT = mybir.ActivationFunctionType

P = 128
PACK = 4
QUADRANTS = 4
LIST_ROWS = 16
WIDE = 2 * S
HALF = S // 2
LOW, HIGH, ALL = slice(0, HALF), slice(HALF, S), slice(0, S)
LAST = PACK - 1
VECTOR_SCATTER_SHARE = 128
SCALAR_WEAVE_COLS = 192
WEAVE_RUN = 4


def entries(list_tile, cols):
    return list_tile[:, cols.start // LIST_ROWS : cols.stop // LIST_ROWS]


def tile_picked_candesdedb_none_p_kernel(
    tc, x_words, x_scales, w1, tau, gs, sl, th, offs, n1, n2, cand, n3, n4, out
):
    nc = tc.nc
    with ExitStack() as ctx:
        keep = ctx.enter_context(tc.tile_pool(name="keep", bufs=1))
        psum = ctx.enter_context(tc.psum_pool(name="psum", bufs=1))

        def load_list(src, name):
            dst = keep.tile([P, S // LIST_ROWS], U16, name=name)
            nc.sync.dma_start(dst[:], src)
            return dst

        def load_row_values(src, name):
            dst = keep.tile([P, PACK], F32, name=name)
            nc.sync.dma_start(dst[:], src.rearrange("(p t) o -> p (t o)", t=PACK))
            return dst

        table_scales = keep.tile([P, T], U8, name="table_scales", align_bytes=64)
        nc.vector.memset(table_scales[:].bitcast(I32), 0)
        offs_sb = load_list(offs, "offs_sb")
        cand_sb = load_list(cand, "cand_sb")
        w_rows = w1.rearrange("(p j) c -> p j c", j=PACK)
        w_raw = [keep.tile([P, PACK, H // 2], F32, name=f"w_raw{h}") for h in range(2)]
        table_words = keep.tile([P, T], U32, name="table_words", align_bytes=64)
        nc.sync.dma_start(w_raw[0][:], w_rows[:, :, : H // 2])
        for q in range(QUADRANTS):
            nc.sync.dma_start(
                table_scales[32 * q : 32 * q + 4, :].bitcast(I32), x_scales[0, 4 * q : 4 * q + 4, :].bitcast(I32)
            )
        nc.sync.dma_start(w_raw[1][:], w_rows[:, :, H // 2 :])
        nc.sync.dma_start(table_words[:].bitcast(I32), x_words[0].rearrange("p n t -> p (n t)").bitcast(I32))
        tau_sb = load_row_values(tau, "tau_sb")
        n1_sb = load_list(n1, "n1_sb")
        gs_sb = load_row_values(gs, "gs_sb")
        n2_sb = load_list(n2, "n2_sb")
        sl_sb = load_row_values(sl, "sl_sb")
        th_sb = load_row_values(th, "th_sb")
        n3_sb = load_list(n3, "n3_sb")
        n4_sb = load_list(n4, "n4_sb")

        xq_scales = keep.tile([P, S], U8, name="xq_scales", align_bytes=64)
        xq_words = keep.tile([P, S], U32, name="xq_words", align_bytes=64)
        xc_scales = keep.tile([P, C], U8, name="xc_scales", align_bytes=64)
        xc_words = keep.tile([P, C], U32, name="xc_words", align_bytes=64)
        nc.vector.tensor_copy(xq_scales[:], table_scales[:].indirect(offs_sb[:]))
        nc.vector.tensor_copy(
            xc_scales[:].rearrange("p (t m) -> p m t", t=PACK), table_scales[:].indirect(cand_sb[:])
        )

        w_woven = keep.tile([P, PACK, P, PACK], BF16, name="w_woven", align_bytes=64)
        for h in range(2):
            nc.scalar.copy(
                w_woven[:, :, h * P // 2 : (h + 1) * P // 2, :].rearrange("p t m j -> p m j t"),
                w_raw[h][:].rearrange("p j (m t) -> p m j t", t=PACK),
            )
        w_words = keep.tile([P, H], U32, name="w_words", align_bytes=64)
        w_scales = keep.tile([P, H], U8, name="w_scales", align_bytes=64)

        half_gs = keep.tile([P, PACK], F32, name="half_gs")
        twice_gs = keep.tile([P, PACK], F32, name="twice_gs")
        minus_tau = keep.tile([P, PACK], F32, name="minus_tau")
        minus_th = keep.tile([P, PACK], F32, name="minus_th")
        sig_bias = keep.tile([P, PACK], F32, name="sig_bias")
        nc.gpsimd.tensor_scalar(minus_tau[:], tau_sb[:], -1.0, 0.0, ALU.mult, ALU.add)
        nc.gpsimd.tensor_scalar(half_gs[:], gs_sb[:], 0.5, 0.0, ALU.mult, ALU.add)
        nc.gpsimd.tensor_scalar(twice_gs[:], gs_sb[:], 2.0, 0.0, ALU.mult, ALU.add)
        nc.gpsimd.tensor_scalar(minus_th[:], th_sb[:], -1.0, 0.0, ALU.mult, ALU.add)
        nc.gpsimd.tensor_tensor(sig_bias[:], minus_th[:], sl_sb[:], ALU.mult)

        for t in range(PACK):
            places = slice(t * P, (t + 1) * P)
            nc.vector.quantize_mx(
                out=w_words[:, places].bitcast(FP8X4),
                scales=w_scales[:, places],
                in_=w_woven[:, t, :, :].rearrange("p m j -> p (m j)"),
            )
        nc.vector.tensor_copy(xq_words[:], table_words[:].indirect(offs_sb[:]))
        nc.vector.tensor_copy(
            xc_words[:].rearrange("p (t m) -> p m t", t=PACK), table_words[:].indirect(cand_sb[:])
        )

        y_bank = [psum.tile([P, S], F32, name=f"y_bank{t}", tag=f"bank{t}") for t in range(PACK)]
        for t in range(PACK):
            places = slice(t * P, (t + 1) * P)
            nc.tensor.matmul_mx(
                out=y_bank[t][:],
                lhsT=w_words[:, places].bitcast(FP8X4),
                lhsT_scale=w_scales[:, places],
                rhs=xq_words[:].bitcast(FP8X4),
                rhs_scale=xq_scales[:],
                start=True,
                stop=True,
            )

        y = [keep.tile([P, WIDE], F32, name=f"y{t}") for t in range(PACK)]
        ea = [keep.tile([P, S], F32, name=f"ea{t}", tag=f"ea{t}", align_bytes=64) for t in range(PACK)]
        ds = [keep.tile([P, S if t in (1, 2) else WIDE], F32, name=f"ds{t}") for t in range(PACK)]
        y_part = [keep.tile([P, S], F32, name=f"y_part{t}") for t in range(LAST)]
        for t in range(PACK):
            top = keep.tile([P, 1], F32, name=f"top{t}")
            exp_bias = keep.tile([P, 1], F32, name=f"exp_bias{t}")
            nc.vector.tensor_scalar(y[t][:, ALL], y_bank[t][:], 1.0, None, ALU.mult, ALU.max, accum_out=top[:])
            nc.scalar.activation(exp_bias[:], top[:], ACT.Copy, scale=minus_tau[:, t : t + 1])
            if t < LAST:
                nc.gpsimd.tensor_scalar(y_part[t][:], y[t][:, ALL], half_gs[:, t : t + 1], 0.0, ALU.mult, ALU.add)
            nc.scalar.activation(
                ea[t][:], y[t][:].indirect(n1_sb[:]), ACT.Exp, bias=exp_bias[:], scale=tau_sb[:, t : t + 1]
            )

        def scatter_on_vector(t, cols):
            nc.vector.tensor_tensor(ds[t][:].indirect(entries(n2_sb, cols)), y[t][:, cols], ea[t][:, cols], ALU.mult)

        def product(t, cols):
            sm = keep.tile([P, S], F32, name=f"sm{t}")
            nc.vector.tensor_tensor(sm[:, cols], y[t][:, cols], ea[t][:, cols], ALU.mult)
            return sm

        def scatter_on_scalar(t, sm, first):
            for cols in (slice(first, HALF), HIGH):
                nc.scalar.activation(ds[t][:].indirect(entries(n2_sb, cols)), sm[:, cols], ACT.Copy)

        scatter_on_vector(0, ALL)
        scatter_on_scalar(1, product(1, ALL), 0)
        sm2 = product(2, slice(VECTOR_SCATTER_SHARE, S))
        scatter_on_vector(2, slice(0, VECTOR_SCATTER_SHARE))
        scatter_on_scalar(2, sm2, VECTOR_SCATTER_SHARE)
        scatter_on_vector(LAST, ALL)

        def combine(t, cols):
            nc.vector.scalar_tensor_tensor(
                z_rows[:, t, cols], ds[t][:, cols], twice_gs[:, t : t + 1], y_part[t][:, cols], ALU.mult, ALU.subtract
            )

        y_part.append(keep.tile([P, S], F32, name="y_part3", tag="ea1", align_bytes=64))
        nc.vector.tensor_scalar(y_part[LAST][:], y[LAST][:, ALL], half_gs[:, LAST : LAST + 1], None, ALU.mult)
        z_rows = keep.tile([P, PACK, S], BF16, name="z_rows", tag="ea2", align_bytes=64)
        for t in (0, LAST, 1):
            combine(t, ALL)
        for cols in (LOW, HIGH):
            combine(2, cols)

        z_woven = keep.tile([P, S, PACK], BF16, name="z_woven", align_bytes=64)
        z_words = keep.tile([P, S], U32, name="z_words", align_bytes=64)
        z_scales = keep.tile([P, S], U8, name="z_scales", align_bytes=64)
        s = [keep.tile([P, WIDE], F32, name=f"s{t}") for t in range(PACK)]

        def weave(copy, c0, c1):
            copy(
                z_woven[:, c0:c1, :].rearrange("p (c i) t -> p c t i", i=WEAVE_RUN),
                z_rows[:, :, c0:c1].rearrange("p t (c i) -> p c t i", i=WEAVE_RUN),
            )

        def score(t, cols, bank):
            places = slice(t * P, (t + 1) * P)
            acc = psum.tile([P, cols.stop - cols.start], F32, name=f"s_bank{bank}", tag=f"bank{bank}")
            nc.tensor.matmul_mx(
                out=acc[:],
                lhsT=xc_words[:, places].bitcast(FP8X4),
                lhsT_scale=xc_scales[:, places],
                rhs=z_words[:, cols].bitcast(FP8X4),
                rhs_scale=z_scales[:, cols],
                start=True,
                stop=True,
            )
            return acc

        weave(nc.scalar.copy, 0, SCALAR_WEAVE_COLS)
        warm_up = keep.tile([P, 1], F32, name="warm_up")
        nc.scalar.activation(warm_up[:], z_woven[:, 0, 0:1], ACT.Sigmoid)
        weave(nc.vector.tensor_copy, HALF, S)
        weave(nc.vector.tensor_copy, SCALAR_WEAVE_COLS, HALF)
        first_banks = []
        for bank, cols in enumerate((HIGH, LOW)):
            nc.vector.quantize_mx(
                out=z_words[:, cols].bitcast(FP8X4),
                scales=z_scales[:, cols],
                in_=z_woven[:, cols, :].rearrange("p c t -> p (c t)"),
            )
            first_banks.append((cols, score(0, cols, bank)))
        s_bank = {t: score(t, ALL, PACK + t) for t in range(1, PACK)}

        out_rows = out.rearrange("(p t) c -> p t c", t=PACK)
        sg = [keep.tile([P, WIDE], F32, name=f"sg{t}") for t in range(PACK)]
        sg2_duplicate = keep.tile([P, S], F32, name="sg2_duplicate")
        sg3_fetched = keep.tile([P, S], F32, name="sg3_fetched")
        diff = [keep.tile([P, S], F32, name=f"diff{t}") for t in range(PACK)]
        res = [keep.tile([P, S], F32, name=f"res{t}") for t in range(PACK)]

        def sigmoid(t, cols):
            nc.scalar.activation(
                sg[t][:, cols],
                s[t][:].indirect(entries(n3_sb, cols)),
                ACT.Sigmoid,
                bias=sig_bias[:, t : t + 1],
                scale=sl_sb[:, t : t + 1],
            )

        def fetch_and_subtract(t, duplicate, cols):
            nc.vector.tensor_tensor(
                diff[t][:, cols], sg[t][:].indirect(entries(n4_sb, cols)), duplicate[:, cols], ALU.subtract
            )

        def subtract_last(cols):
            nc.vector.tensor_tensor(diff[LAST][:, cols], sg3_fetched[:, cols], sg[LAST][:, cols], ALU.subtract)

        def finish(t, cols):
            nc.vector.scalar_tensor_tensor(res[t][:, cols], diff[t][:, cols], -1.5, s[t][:, cols], ALU.mult, ALU.mult)
            nc.sync.dma_start(out_rows[:, t, cols], res[t][:, cols])

        for cols, acc in first_banks:
            nc.vector.tensor_scalar(s[0][:, cols], acc[:], 0.0625, None, ALU.mult)
        for t in range(1, LAST):
            nc.vector.tensor_scalar(s[t][:, ALL], s_bank[t][:], 0.0625, None, ALU.mult)
        for cols in (LOW, HIGH):
            sigmoid(0, cols)
        sigmoid(1, ALL)
        sigmoid(2, ALL)
        nc.scalar.activation(s[LAST][:, ALL], s_bank[LAST][:], ACT.Copy, scale=0.0625)
        nc.scalar.copy(sg2_duplicate[:], sg[2][:, ALL])
        sigmoid(LAST, ALL)
        for cols in (LOW, HIGH):
            nc.scalar.activation(sg3_fetched[:, cols], sg[LAST][:].indirect(entries(n4_sb, cols)), ACT.Copy)

        sg0_duplicate = keep.tile([P, S], F32, name="sg0_duplicate", tag="vector_duplicate")
        for cols in (LOW, HIGH):
            nc.vector.tensor_copy(sg0_duplicate[:, cols], sg[0][:, cols])
        for cols in (LOW, HIGH):
            fetch_and_subtract(0, sg0_duplicate, cols)
        sg1_duplicate = keep.tile([P, S], F32, name="sg1_duplicate", tag="vector_duplicate")
        nc.vector.tensor_copy(sg1_duplicate[:], sg[1][:, ALL])
        finish(0, ALL)
        fetch_and_subtract(1, sg1_duplicate, ALL)
        fetch_and_subtract(2, sg2_duplicate, ALL)
        finish(1, ALL)
        subtract_last(LOW)
        finish(2, ALL)
        subtract_last(HIGH)
        for cols in (LOW, HIGH):
            finish(LAST, cols)
